import numpy as np, ml_dtypes
CORES = [16,17,18,19,150,151]
N = 6
QP = 32
def setup_inputs(rng):
    return {"q": rng.standard_normal((N, 128, QP), dtype=np.float32).astype(ml_dtypes.bfloat16), "k": rng.standard_normal((N, 128, 128), dtype=np.float32).astype(ml_dtypes.bfloat16), "v": rng.standard_normal((N, 128, 128), dtype=np.float32).astype(ml_dtypes.bfloat16)}
def setup_inputs_big(rng):
    d = setup_inputs(rng)
    for k in ("q", "k", "v"): d[k] = (d[k].astype(np.float32) * 1024.0).astype(d[k].dtype)
    return d
def setup_inputs_small(rng):
    d = setup_inputs(rng)
    for k in ("q", "k", "v"): d[k] = (d[k].astype(np.float32) * (1 / 1024.0)).astype(d[k].dtype)
    return d
def setup_inputs_apart(rng):
    d = setup_inputs(rng)
    f = (10.0 ** rng.permutation(np.linspace(-1.5, 1.5, N))).astype(np.float32).reshape(N, 1, 1)
    for k in ("q", "k", "v"): d[k] = (d[k].astype(np.float32) * f).astype(d[k].dtype)
    return d
def reference(q, k, v):
    Q, K, V = q.astype(np.float64), k.astype(np.float64), v.astype(np.float64)
    y = np.zeros((N, 128, QP))
    for r in range(N):
        S = [K[j].T @ Q[r] for j in range(N)]
        m = np.max([s.max(axis=0) for s in S], axis=0)
        y[r] = sum(V[j].T @ np.maximum(S[j] - 0.5 * m, 0.0) for j in range(N))
    return {"y": y.astype(ml_dtypes.bfloat16)}

@@ -1,0 +1,168 @@
+from concourse.bass import DstId, RemoteDMATransfer
+from concourse.mybir import AluOpType
+
+N, QP, KP = 6, 32, 128
+W = 2 * KP
+C = N * QP
+
+SCRATCH = {
+    "kv": ("sbuf", [128, N * W], "bfloat16"),
+    "qs": ("sbuf", [128, QP], "bfloat16"),
+    "erow": ("sbuf", [128, QP * QP], "bfloat16"),
+    "zero": ("sbuf", [128, C], "bfloat16"),
+    "nh": ("sbuf", [128, KP], "bfloat16"),
+    "eye6": ("sbuf", [128, C], "bfloat16"),
+    "tr": ("sbuf", [128, 192], "float32"),
+    "mcol": ("sbuf", [128, 8], "bfloat16"),
+    "mrow": ("sbuf", [128, C], "bfloat16"),
+    "pp": ("sbuf", [128, C], "bfloat16"),
+    "ysb": ("sbuf", [128, QP], "bfloat16"),
+    "sp": ("psum", [128, 512], "float32"),
+    "yp": ("psum", [128, 512], "float32"),
+}
+for _j in range(N):
+    SCRATCH["st%d" % _j] = ("psum", [128, 512], "float32")
+
+SEMAPHORES = ["ld", "ldq", "sent", "c0", "cs", "zi", "im", "ic", "sa", "vx", "mx", "rw", "rc", "bs", "r1", "r2", "ym",
+              "yc", "out"] + ["arr%d" % j for j in range(N)] + ["st%d" % j for j in range(N)]
+
+
+def _place(topo, c):
+    return (topo.host(c), topo.chip(c))
+
+
+def _send_mask(topo, cores, s, d):
+    m = topo.mask(s, d)
+    if _place(topo, s) != _place(topo, d):
+        return m
+    for x in cores:
+        if _place(topo, x) != _place(topo, s):
+            m &= ~topo.mask(s, x)
+    return m
+
+
+def _bits(m):
+    return bin(m).count("1")
+
+
+def rank_program(g, core, T, topo):
+    rank = T.rank_of(core)
+    if rank is None:
+        return
+    cores = list(T.cores)
+    S = T.sem
+    te, ve = g.tensor, g.vector
+    mx_op = AluOpType.max
+
+    def kcols(j):
+        return T.kv[:, W * j:W * j + KP]
+
+    def vcols(j):
+        return T.kv[:, W * j + KP:W * (j + 1)]
+
+    def slot(j):
+        return T.kv[:, W * j:W * (j + 1)]
+
+    near = [c for c in cores if c != core and _place(topo, c) == _place(topo, core)]
+    far = [c for c in cores if _place(topo, c) != _place(topo, core)]
+
+    g.sync.dma_start(kcols(rank), T.k[:, :]).then_inc(S.ld, 16)
+    g.scalar.dma_start(vcols(rank), T.v[:, :]).then_inc(S.ld, 16)
+    g.sync.dma_start(T.qs[:, :], T.q[:, :]).then_inc(S.ldq, 16)
+
+    g.wait_ge(S.ld, 32)
+    sent = 0
+    for dsts in sorted([near, far], key=len, reverse=True):
+        if not dsts:
+            continue
+        m = _send_mask(topo, cores, core, dsts[0])
+        ids = []
+        for d in dsts:
+            rid, pid = topo.addr(d, core)
+            ids.append(DstId(rid=rid, pnc=pid))
+        g.remote_dma_fused([RemoteDMATransfer(dst_ids=ids, dma_engine_mask=m, remote_sem=S["arr%d" % rank],
+                                              srcs=[slot(rank)], dsts=[slot(rank) for _ in dsts], alu_op=0)],
+                           local_sem=S.sent)
+        sent += _bits(m)
+
+    ve.memset(T.erow[0:1, :], 0.0).then_inc(S.c0, 1)
+    ve.memset(T.zero[:, :], 0.0).then_inc(S.cs, 1)
+    ve.memset(T.nh[0:1, :], -0.5).then_inc(S.cs, 1)
+    ve.wait_ge(S.c0, 1)
+    ve.memset(T.erow[0:1, 0:QP * QP:QP + 1], 1.0).then_inc(S.cs, 1)
+    ve.wait_ge(S.cs, 3)
+
+    te.wait_ge(S.cs, 3)
+    te.matmul(T.sp[:, 0:C], T.zero[0:1, 0:KP], T.zero[0:1, 0:C], start=True, stop=False).then_inc(S.zi, 1)
+    for i in range(QP):
+        e = T.erow[0:1, QP * i:QP * (i + 1)]
+        mm = te.matmul(T.yp[0:QP, 0:QP], e, e, start=(i == 0), stop=(i == QP - 1))
+    mm.then_inc(S.im, 1)
+    ve.wait_ge(S.im, 1)
+    for j in range(N):
+        ve.tensor_copy(T.eye6[0:QP, QP * j:QP * (j + 1)], T.yp[0:QP, 0:QP]).then_inc(S.ic, 1)
+
+    order = [rank] + [T.rank_of(c) for c in near] + [T.rank_of(c) for c in far]
+    te.wait_ge(S.zi, 1)
+    te.wait_ge(S.ldq, 16)
+    H = KP // 2
+    halves = [T.tr[0:QP, 0:H], T.tr[0:QP, H:2 * H]]
+    nv = 0
+    for j in order:
+        if j == rank:
+            te.wait_ge(S.ld, 32)
+        else:
+            te.wait_ge(S["arr%d" % j], _bits(_send_mask(topo, cores, cores[j], core)))
+        st = T["st%d" % j]
+        te.matmul(st[0:QP, 0:KP], T.qs[:, :], kcols(j), start=True, stop=True).then_inc(S["st%d" % j], 1)
+        te.matmul(T.sp[:, QP * j:QP * (j + 1)], kcols(j), T.qs[:, :], start=False, stop=False).then_inc(S.sa, 1)
+        ve.wait_ge(S["st%d" % j], 1)
+        for h in range(2):
+            part = st[0:QP, H * h:H * (h + 1)]
+            if nv == 0:
+                ve.tensor_copy(halves[0], part).then_inc(S.vx, 1)
+            else:
+                ve.wait_ge(S.vx, nv)
+                ve.tensor_tensor(halves[nv % 2], part, halves[(nv - 1) % 2], mx_op).then_inc(S.vx, 1)
+            nv += 1
+    cur, width, base = halves[(nv - 1) % 2], H, 2 * H
+    cur_lo = ((nv - 1) % 2) * H
+    while width > 1:
+        width //= 2
+        ve.wait_ge(S.vx, nv)
+        a = T.tr[0:QP, cur_lo:cur_lo + width]
+        b = T.tr[0:QP, cur_lo + width:cur_lo + 2 * width]
+        if width > 1:
+            ve.tensor_tensor(T.tr[0:QP, base:base + width], a, b, mx_op).then_inc(S.vx, 1)
+            nv += 1
+            cur_lo, base = base, base + width
+        else:
+            ve.tensor_tensor(T.mcol[0:QP, 0:1], a, b, mx_op).then_inc(S.mx, 1)
+
+    own = T["st%d" % rank]
+    te.wait_ge(S.ic, N)
+    te.wait_ge(S.mx, 1)
+    te.matmul(own[0:1, 0:C], T.mcol[0:QP, 0:1], T.eye6[0:QP, 0:C], start=True, stop=True).then_inc(S.rw, 1)
+    ve.wait_ge(S.rw, 1)
+    ve.tensor_copy(T.mrow[0:1, 0:C], own[0:1, 0:C]).then_inc(S.rc, 1)
+    te.wait_ge(S.rc, 1)
+    te.wait_ge(S.sa, N)
+    te.matmul(T.sp[:, 0:C], T.nh[0:1, 0:KP], T.mrow[0:1, 0:C], start=False, stop=True).then_inc(S.bs, 1)
+    ve.wait_ge(S.bs, 1)
+    half = C // 2
+    ve.tensor_tensor(T.pp[:, 0:half], T.sp[:, 0:half], T.zero[:, 0:half], mx_op).then_inc(S.r1, 1)
+    ve.tensor_tensor(T.pp[:, half:C], T.sp[:, half:C], T.zero[:, half:C], mx_op).then_inc(S.r2, 1)
+
+    for j in range(N):
+        if j == 0:
+            te.wait_ge(S.r1, 1)
+        if j == N // 2:
+            te.wait_ge(S.r2, 1)
+        mm = te.matmul(T.yp[:, 0:QP], vcols(j), T.pp[:, QP * j:QP * (j + 1)], start=(j == 0), stop=(j == N - 1))
+    mm.then_inc(S.ym, 1)
+    ve.wait_ge(S.ym, 1)
+    ve.tensor_copy(T.ysb[:, :], T.yp[:, 0:QP]).then_inc(S.yc, 1)
+    g.sync.wait_ge(S.yc, 1)
+    g.sync.dma_start(T.y[:, :], T.ysb[:, :]).then_inc(S.out, 16)
+    g.sync.wait_ge(S.out, 16)
+    g.wait_ge(S.sent, sent)

@@ -31,18 +31,63 @@ def _place(topo, c):
     return (topo.host(c), topo.chip(c))
 
 
-def _send_mask(topo, cores, s, d):
-    m = topo.mask(s, d)
-    if _place(topo, s) != _place(topo, d):
-        return m
-    for x in cores:
-        if _place(topo, x) != _place(topo, s):
-            m &= ~topo.mask(s, x)
-    return m
-
-
 def _bits(m):
     return bin(m).count("1")
+
+
+def _plan(topo, cores):
+    groups = {}
+    for c in cores:
+        groups.setdefault(_place(topo, c), []).append(c)
+    rk = {c: i for i, c in enumerate(cores)}
+    sends = {c: [] for c in cores}
+    got = {c: {"near": [], "far": [], "fwd": []} for c in cores}
+    passes = {c: [] for c in cores}
+    for c in cores:
+        L = groups[_place(topo, c)]
+        i, a, r = L.index(c), len(L), rk[c]
+        sem = "arr%d" % r
+        near = [x for x in L if x != c]
+        full = topo.mask(c, near[0])
+        off = full
+        targets = []
+        for p, G in groups.items():
+            if p == _place(topo, c):
+                continue
+            b = len(G)
+            off &= topo.mask(c, G[0])
+            if a <= b:
+                tg = [x for x in range(b) if x % a == i]
+                for x in tg:
+                    blk = [G[y] for y in range((x // a) * a, (x // a + 1) * a) if y != x]
+                    passes[G[x]].append((r, r + 1, blk))
+            else:
+                n = a // b
+                tg = [i // n]
+                if i % n == 0:
+                    passes[G[tg[0]]].append((r, r + n, [y for y in G if y != G[tg[0]]]))
+            targets += [G[x] for x in tg]
+        rest = full & ~off
+        sends[c].append(([], [(off, targets, r, r + 1, sem)]))
+        for d in targets:
+            got[d]["far"].append((sem, _bits(off), [r]))
+        load = {off: len(targets), rest: 0}
+        deal = {off: [], rest: []}
+        for d in near:
+            m = rest if load[rest] <= load[off] else off
+            deal[m].append(d)
+            load[m] += 1
+            got[d]["near"].append((sem, _bits(m), [r]))
+        sends[c].append(([], [(m, deal[m], r, r + 1, sem) for m in (rest, off) if deal[m]]))
+    for c in cores:
+        for lo, hi, dsts in passes[c]:
+            full = topo.mask(c, dsts[0])
+            waits = [(s, n) for s, n, sl in got[c]["far"] if lo <= sl[0] < hi]
+            sends[c].append((waits, [(full, dsts, lo, hi, "arr%d" % lo)]))
+            for d in dsts:
+                got[d]["fwd"].append(("arr%d" % lo, _bits(full), list(range(lo, hi))))
+    recvs = {c: got[c]["near"] + got[c]["far"] + got[c]["fwd"] for c in cores}
+    return sends, recvs
 
 
 def rank_program(g, core, T, topo):
@@ -53,6 +98,7 @@ def rank_program(g, core, T, topo):
     S = T.sem
     te, ve = g.tensor, g.vector
     mx_op = AluOpType.max
+    sends, recvs = _plan(topo, cores)
 
     def kcols(j):
         return T.kv[:, W * j:W * j + KP]
@@ -60,30 +106,26 @@ def rank_program(g, core, T, topo):
     def vcols(j):
         return T.kv[:, W * j + KP:W * (j + 1)]
 
-    def slot(j):
-        return T.kv[:, W * j:W * (j + 1)]
-
-    near = [c for c in cores if c != core and _place(topo, c) == _place(topo, core)]
-    far = [c for c in cores if _place(topo, c) != _place(topo, core)]
-
     g.sync.dma_start(kcols(rank), T.k[:, :]).then_inc(S.ld, 16)
     g.scalar.dma_start(vcols(rank), T.v[:, :]).then_inc(S.ld, 16)
     g.sync.dma_start(T.qs[:, :], T.q[:, :]).then_inc(S.ldq, 16)
 
     g.wait_ge(S.ld, 32)
     sent = 0
-    for dsts in sorted([near, far], key=len, reverse=True):
-        if not dsts:
-            continue
-        m = _send_mask(topo, cores, core, dsts[0])
-        ids = []
-        for d in dsts:
-            rid, pid = topo.addr(d, core)
-            ids.append(DstId(rid=rid, pnc=pid))
-        g.remote_dma_fused([RemoteDMATransfer(dst_ids=ids, dma_engine_mask=m, remote_sem=S["arr%d" % rank],
-                                              srcs=[slot(rank)], dsts=[slot(rank) for _ in dsts], alu_op=0)],
-                           local_sem=S.sent)
-        sent += _bits(m)
+    for waits, transfers in sends[core]:
+        for s, n in waits:
+            g.wait_ge(S[s], n)
+        trs = []
+        for m, dsts, lo, hi, s in transfers:
+            ids = []
+            for d in dsts:
+                rid, pid = topo.addr(d, core)
+                ids.append(DstId(rid=rid, pnc=pid))
+            ap = T.kv[:, W * lo:W * hi]
+            trs.append(RemoteDMATransfer(dst_ids=ids, dma_engine_mask=m, remote_sem=S[s], srcs=[ap],
+                                         dsts=[ap for _ in dsts], alu_op=0))
+            sent += _bits(m)
+        g.remote_dma_fused(trs, local_sem=S.sent)
 
     ve.memset(T.erow[0:1, :], 0.0).then_inc(S.c0, 1)
     ve.memset(T.zero[:, :], 0.0).then_inc(S.cs, 1)
@@ -102,30 +144,27 @@ def rank_program(g, core, T, topo):
     for j in range(N):
         ve.tensor_copy(T.eye6[0:QP, QP * j:QP * (j + 1)], T.yp[0:QP, 0:QP]).then_inc(S.ic, 1)
 
-    order = [rank] + [T.rank_of(c) for c in near] + [T.rank_of(c) for c in far]
     te.wait_ge(S.zi, 1)
     te.wait_ge(S.ldq, 16)
     H = KP // 2
     halves = [T.tr[0:QP, 0:H], T.tr[0:QP, H:2 * H]]
     nv = 0
-    for j in order:
-        if j == rank:
-            te.wait_ge(S.ld, 32)
-        else:
-            te.wait_ge(S["arr%d" % j], _bits(_send_mask(topo, cores, cores[j], core)))
-        st = T["st%d" % j]
-        te.matmul(st[0:QP, 0:KP], T.qs[:, :], kcols(j), start=True, stop=True).then_inc(S["st%d" % j], 1)
-        te.matmul(T.sp[:, QP * j:QP * (j + 1)], kcols(j), T.qs[:, :], start=False, stop=False).then_inc(S.sa, 1)
-        ve.wait_ge(S["st%d" % j], 1)
-        for h in range(2):
-            part = st[0:QP, H * h:H * (h + 1)]
-            if nv == 0:
-                ve.tensor_copy(halves[0], part).then_inc(S.vx, 1)
-            else:
-                ve.wait_ge(S.vx, nv)
-                ve.tensor_tensor(halves[nv % 2], part, halves[(nv - 1) % 2], mx_op).then_inc(S.vx, 1)
-            nv += 1
-    cur, width, base = halves[(nv - 1) % 2], H, 2 * H
+    for s, n, slots in [("ld", 32, [rank])] + recvs[core]:
+        te.wait_ge(S[s], n)
+        for j in slots:
+            st = T["st%d" % j]
+            te.matmul(st[0:QP, 0:KP], T.qs[:, :], kcols(j), start=True, stop=True).then_inc(S["st%d" % j], 1)
+            te.matmul(T.sp[:, QP * j:QP * (j + 1)], kcols(j), T.qs[:, :], start=False, stop=False).then_inc(S.sa, 1)
+            ve.wait_ge(S["st%d" % j], 1)
+            for h in range(2):
+                part = st[0:QP, H * h:H * (h + 1)]
+                if nv == 0:
+                    ve.tensor_copy(halves[0], part).then_inc(S.vx, 1)
+                else:
+                    ve.wait_ge(S.vx, nv)
+                    ve.tensor_tensor(halves[nv % 2], part, halves[(nv - 1) % 2], mx_op).then_inc(S.vx, 1)
+                nv += 1
+    width, base = H, 2 * H
     cur_lo = ((nv - 1) % 2) * H
     while width > 1:
         width //= 2

@@ -3,28 +3,44 @@ from concourse.mybir import AluOpType
 
 N, QP, KP = 6, 32, 128
 W = 2 * KP
-C = N * QP
+HN = N // 2
+HC = HN * QP
 
 SCRATCH = {
     "kv": ("sbuf", [128, N * W], "bfloat16"),
     "qs": ("sbuf", [128, QP], "bfloat16"),
     "erow": ("sbuf", [128, QP * QP], "bfloat16"),
-    "zero": ("sbuf", [128, C], "bfloat16"),
+    "zero": ("sbuf", [128, KP], "bfloat16"),
     "nh": ("sbuf", [128, KP], "bfloat16"),
-    "eye6": ("sbuf", [128, C], "bfloat16"),
+    "eye3": ("sbuf", [128, HC], "bfloat16"),
     "tr": ("sbuf", [128, 192], "float32"),
     "mcol": ("sbuf", [128, 8], "bfloat16"),
-    "mrow": ("sbuf", [128, C], "bfloat16"),
-    "pp": ("sbuf", [128, C], "bfloat16"),
+    "mrow": ("sbuf", [128, HC], "bfloat16"),
+    "pp": ("sbuf", [128, 2 * HC], "bfloat16"),
     "ysb": ("sbuf", [128, QP], "bfloat16"),
-    "sp": ("psum", [128, 512], "float32"),
+    "sp0": ("psum", [128, 512], "float32"),
+    "sp1": ("psum", [128, 512], "float32"),
     "yp": ("psum", [128, 512], "float32"),
 }
-for _j in range(N):
+for _j in range(1, N):
     SCRATCH["st%d" % _j] = ("psum", [128, 512], "float32")
 
-SEMAPHORES = ["ld", "ldq", "sent", "c0", "cs", "zi", "im", "ic", "sa", "vx", "mx", "rw", "rc", "bs", "r1", "r2", "ym",
-              "yc", "out"] + ["arr%d" % j for j in range(N)] + ["st%d" % j for j in range(N)]
+SEMAPHORES = ["ldk", "ldv", "ldq", "sent", "c0", "cs", "zi", "im", "ic", "sa", "vx", "mx", "rw", "rc", "b0", "b1", "r0",
+              "r1", "ym", "yc", "out"] + [p + str(j) for p in ("arr", "ka", "va", "st") for j in range(N)]
+
+
+def _kc(j):
+    b = (j // 2) * 2 * W
+    return (b, b + KP) if j % 2 == 0 else (b + 3 * KP, b + 4 * KP)
+
+
+def _vc(j):
+    b = (j // 2) * 2 * W
+    return (b + KP, b + 2 * KP) if j % 2 == 0 else (b + 2 * KP, b + 3 * KP)
+
+
+def _sc(j):
+    return (min(_kc(j)[0], _vc(j)[0]), max(_kc(j)[1], _vc(j)[1]))
 
 
 def _place(topo, c):
@@ -35,59 +51,57 @@ def _bits(m):
     return bin(m).count("1")
 
 
+def _halves(m):
+    e = [1 << x for x in range(m.bit_length()) if (m >> x) & 1]
+    return sum(e[:len(e) // 2]), sum(e[len(e) // 2:])
+
+
 def _plan(topo, cores):
     groups = {}
     for c in cores:
         groups.setdefault(_place(topo, c), []).append(c)
     rk = {c: i for i, c in enumerate(cores)}
-    sends = {c: [] for c in cores}
-    got = {c: {"near": [], "far": [], "fwd": []} for c in cores}
-    passes = {c: [] for c in cores}
+    sends, kr, vr, far, fwd, nearr, restm = {}, {}, {}, {}, {}, {}, {}
+    for c in cores:
+        kr[c], vr[c], far[c], fwd[c], nearr[c] = {rk[c]: ("ldk", 16)}, {rk[c]: ("ldv", 16)}, [], [], []
     for c in cores:
         L = groups[_place(topo, c)]
-        i, a, r = L.index(c), len(L), rk[c]
-        sem = "arr%d" % r
-        near = [x for x in L if x != c]
+        G = [x for x in cores if x not in L]
+        i, a, b, r = L.index(c), len(L), len(G), rk[c]
+        near = L[i + 1:] + L[:i]
         full = topo.mask(c, near[0])
-        off = full
-        targets = []
-        for p, G in groups.items():
-            if p == _place(topo, c):
-                continue
-            b = len(G)
-            off &= topo.mask(c, G[0])
-            if a <= b:
-                tg = [x for x in range(b) if x % a == i]
-                for x in tg:
-                    blk = [G[y] for y in range((x // a) * a, (x // a + 1) * a) if y != x]
-                    passes[G[x]].append((r, r + 1, blk))
-            else:
-                n = a // b
-                tg = [i // n]
-                if i % n == 0:
-                    passes[G[tg[0]]].append((r, r + n, [y for y in G if y != G[tg[0]]]))
-            targets += [G[x] for x in tg]
+        off = full & topo.mask(c, G[0])
         rest = full & ~off
-        sends[c].append(([], [(off, targets, r, r + 1, sem)]))
-        for d in targets:
-            got[d]["far"].append((sem, _bits(off), [r]))
-        load = {off: len(targets), rest: 0}
-        deal = {off: [], rest: []}
+        restm[c] = rest
+        tg = [G[x] for x in range(b) if x % a == i] if a <= b else [G[i // (a // b)]]
+        sends[c] = [([("ldk", 16), ("ldv", 16)], [(rest, near, _sc(r), "arr%d" % r)]),
+                    ([], [(off, tg, _kc(r), "ka%d" % r)]),
+                    ([], [(off, tg, _vc(r), "va%d" % r)])]
+        for d in tg:
+            kr[d][r], vr[d][r] = ("ka%d" % r, _bits(off)), ("va%d" % r, _bits(off))
+            far[d].append(r)
         for d in near:
-            m = rest if load[rest] <= load[off] else off
-            deal[m].append(d)
-            load[m] += 1
-            got[d]["near"].append((sem, _bits(m), [r]))
-        sends[c].append(([], [(m, deal[m], r, r + 1, sem) for m in (rest, off) if deal[m]]))
+            kr[d][r] = vr[d][r] = ("arr%d" % r, _bits(rest))
+            nearr[d].append(r)
     for c in cores:
-        for lo, hi, dsts in passes[c]:
-            full = topo.mask(c, dsts[0])
-            waits = [(s, n) for s, n, sl in got[c]["far"] if lo <= sl[0] < hi]
-            sends[c].append((waits, [(full, dsts, lo, hi, "arr%d" % lo)]))
-            for d in dsts:
-                got[d]["fwd"].append(("arr%d" % lo, _bits(full), list(range(lo, hi))))
-    recvs = {c: got[c]["near"] + got[c]["far"] + got[c]["fwd"] for c in cores}
-    return sends, recvs
+        L = groups[_place(topo, c)]
+        held = sorted(far[c])
+        who = {}
+        for r in held:
+            holders = [x for x in L if r in far[x]]
+            lacking = [x for x in L if r not in far[x]]
+            who[r] = lacking[holders.index(c)::len(holders)]
+        rest = restm[c]
+        masks = [rest] if len(held) == 1 else list(_halves(rest))
+        sends[c].append(([kr[c][r] for r in held], [(masks[t], who[r], _kc(r), "ka%d" % r) for t, r in enumerate(held)]))
+        cols = (min(_vc(r)[0] for r in held), max(_vc(r)[1] for r in held))
+        sends[c].append(([vr[c][r] for r in held], [(rest, who[held[0]], cols, "va%d" % held[0])]))
+        for t, r in enumerate(held):
+            for d in who[r]:
+                kr[d][r], vr[d][r] = ("ka%d" % r, _bits(masks[t])), ("va%d" % held[0], _bits(rest))
+                fwd[d].append(r)
+    order = {c: [rk[c]] + nearr[c] + far[c] + fwd[c] for c in cores}
+    return sends, kr, vr, order
 
 
 def rank_program(g, core, T, topo):
@@ -98,32 +112,29 @@ def rank_program(g, core, T, topo):
     S = T.sem
     te, ve = g.tensor, g.vector
     mx_op = AluOpType.max
-    sends, recvs = _plan(topo, cores)
+    sends, kr, vr, order = _plan(topo, cores)
+    sends, kr, vr, order = sends[core], kr[core], vr[core], order[core]
+    sp = [T.sp0, T.sp1]
 
-    def kcols(j):
-        return T.kv[:, W * j:W * j + KP]
+    def cols(cc):
+        return T.kv[:, cc[0]:cc[1]]
 
-    def vcols(j):
-        return T.kv[:, W * j + KP:W * (j + 1)]
-
-    g.sync.dma_start(kcols(rank), T.k[:, :]).then_inc(S.ld, 16)
-    g.scalar.dma_start(vcols(rank), T.v[:, :]).then_inc(S.ld, 16)
+    g.sync.dma_start(cols(_kc(rank)), T.k[:, :]).then_inc(S.ldk, 16)
+    g.scalar.dma_start(cols(_vc(rank)), T.v[:, :]).then_inc(S.ldv, 16)
     g.sync.dma_start(T.qs[:, :], T.q[:, :]).then_inc(S.ldq, 16)
 
-    g.wait_ge(S.ld, 32)
     sent = 0
-    for waits, transfers in sends[core]:
+    for waits, transfers in sends:
         for s, n in waits:
             g.wait_ge(S[s], n)
         trs = []
-        for m, dsts, lo, hi, s in transfers:
+        for m, dsts, cc, s in transfers:
             ids = []
             for d in dsts:
                 rid, pid = topo.addr(d, core)
                 ids.append(DstId(rid=rid, pnc=pid))
-            ap = T.kv[:, W * lo:W * hi]
-            trs.append(RemoteDMATransfer(dst_ids=ids, dma_engine_mask=m, remote_sem=S[s], srcs=[ap],
-                                         dsts=[ap for _ in dsts], alu_op=0))
+            trs.append(RemoteDMATransfer(dst_ids=ids, dma_engine_mask=m, remote_sem=S[s], srcs=[cols(cc)],
+                                         dsts=[cols(cc) for _ in dsts], alu_op=0))
             sent += _bits(m)
         g.remote_dma_fused(trs, local_sem=S.sent)
 
@@ -135,35 +146,37 @@ def rank_program(g, core, T, topo):
     ve.wait_ge(S.cs, 3)
 
     te.wait_ge(S.cs, 3)
-    te.matmul(T.sp[:, 0:C], T.zero[0:1, 0:KP], T.zero[0:1, 0:C], start=True, stop=False).then_inc(S.zi, 1)
+    for h in range(2):
+        te.matmul(sp[h][:, 0:HC], T.zero[0:1, 0:KP], T.zero[0:1, 0:HC], start=True, stop=False).then_inc(S.zi, 1)
     for i in range(QP):
         e = T.erow[0:1, QP * i:QP * (i + 1)]
         mm = te.matmul(T.yp[0:QP, 0:QP], e, e, start=(i == 0), stop=(i == QP - 1))
     mm.then_inc(S.im, 1)
     ve.wait_ge(S.im, 1)
-    for j in range(N):
-        ve.tensor_copy(T.eye6[0:QP, QP * j:QP * (j + 1)], T.yp[0:QP, 0:QP]).then_inc(S.ic, 1)
+    for j in range(HN):
+        ve.tensor_copy(T.eye3[0:QP, QP * j:QP * (j + 1)], T.yp[0:QP, 0:QP]).then_inc(S.ic, 1)
 
-    te.wait_ge(S.zi, 1)
+    te.wait_ge(S.zi, 2)
+    te.wait_ge(S.ic, HN)
     te.wait_ge(S.ldq, 16)
     H = KP // 2
     halves = [T.tr[0:QP, 0:H], T.tr[0:QP, H:2 * H]]
     nv = 0
-    for s, n, slots in [("ld", 32, [rank])] + recvs[core]:
-        te.wait_ge(S[s], n)
-        for j in slots:
-            st = T["st%d" % j]
-            te.matmul(st[0:QP, 0:KP], T.qs[:, :], kcols(j), start=True, stop=True).then_inc(S["st%d" % j], 1)
-            te.matmul(T.sp[:, QP * j:QP * (j + 1)], kcols(j), T.qs[:, :], start=False, stop=False).then_inc(S.sa, 1)
-            ve.wait_ge(S["st%d" % j], 1)
-            for h in range(2):
-                part = st[0:QP, H * h:H * (h + 1)]
-                if nv == 0:
-                    ve.tensor_copy(halves[0], part).then_inc(S.vx, 1)
-                else:
-                    ve.wait_ge(S.vx, nv)
-                    ve.tensor_tensor(halves[nv % 2], part, halves[(nv - 1) % 2], mx_op).then_inc(S.vx, 1)
-                nv += 1
+    for t, j in enumerate(order):
+        te.wait_ge(S[kr[j][0]], kr[j][1])
+        st = T.yp if t == 0 else T["st%d" % t]
+        c0 = QP * (t % HN)
+        te.matmul(st[0:QP, 0:KP], T.qs[:, :], cols(_kc(j)), start=True, stop=True).then_inc(S["st%d" % t], 1)
+        te.matmul(sp[t // HN][:, c0:c0 + QP], cols(_kc(j)), T.qs[:, :], start=False, stop=False).then_inc(S.sa, 1)
+        ve.wait_ge(S["st%d" % t], 1)
+        for h in range(2):
+            part = st[0:QP, H * h:H * (h + 1)]
+            if nv == 0:
+                ve.tensor_copy(halves[0], part).then_inc(S.vx, 1)
+            else:
+                ve.wait_ge(S.vx, nv)
+                ve.tensor_tensor(halves[nv % 2], part, halves[(nv - 1) % 2], mx_op).then_inc(S.vx, 1)
+            nv += 1
     width, base = H, 2 * H
     cur_lo = ((nv - 1) % 2) * H
     while width > 1:
@@ -178,26 +191,21 @@ def rank_program(g, core, T, topo):
         else:
             ve.tensor_tensor(T.mcol[0:QP, 0:1], a, b, mx_op).then_inc(S.mx, 1)
 
-    own = T["st%d" % rank]
-    te.wait_ge(S.ic, N)
     te.wait_ge(S.mx, 1)
-    te.matmul(own[0:1, 0:C], T.mcol[0:QP, 0:1], T.eye6[0:QP, 0:C], start=True, stop=True).then_inc(S.rw, 1)
+    te.matmul(T.st1[0:1, 0:HC], T.mcol[0:QP, 0:1], T.eye3[0:QP, 0:HC], start=True, stop=True).then_inc(S.rw, 1)
     ve.wait_ge(S.rw, 1)
-    ve.tensor_copy(T.mrow[0:1, 0:C], own[0:1, 0:C]).then_inc(S.rc, 1)
+    ve.tensor_copy(T.mrow[0:1, 0:HC], T.st1[0:1, 0:HC]).then_inc(S.rc, 1)
     te.wait_ge(S.rc, 1)
     te.wait_ge(S.sa, N)
-    te.matmul(T.sp[:, 0:C], T.nh[0:1, 0:KP], T.mrow[0:1, 0:C], start=False, stop=True).then_inc(S.bs, 1)
-    ve.wait_ge(S.bs, 1)
-    half = C // 2
-    ve.tensor_tensor(T.pp[:, 0:half], T.sp[:, 0:half], T.zero[:, 0:half], mx_op).then_inc(S.r1, 1)
-    ve.tensor_tensor(T.pp[:, half:C], T.sp[:, half:C], T.zero[:, half:C], mx_op).then_inc(S.r2, 1)
-
-    for j in range(N):
-        if j == 0:
-            te.wait_ge(S.r1, 1)
-        if j == N // 2:
-            te.wait_ge(S.r2, 1)
-        mm = te.matmul(T.yp[:, 0:QP], vcols(j), T.pp[:, QP * j:QP * (j + 1)], start=(j == 0), stop=(j == N - 1))
+    for h in range(2):
+        te.matmul(sp[h][:, 0:HC], T.nh[0:1, 0:KP], T.mrow[0:1, 0:HC], start=False, stop=True).then_inc(S["b%d" % h], 1)
+        ve.wait_ge(S["b%d" % h], 1)
+        ve.tensor_tensor(T.pp[:, HC * h:HC * (h + 1)], sp[h][:, 0:HC], T.zero[:, 0:HC], mx_op).then_inc(S["r%d" % h], 1)
+    for t, j in enumerate(order):
+        if t % HN == 0:
+            te.wait_ge(S["r%d" % (t // HN)], 1)
+        te.wait_ge(S[vr[j][0]], vr[j][1])
+        mm = te.matmul(T.yp[:, 0:QP], cols(_vc(j)), T.pp[:, QP * t:QP * (t + 1)], start=(t == 0), stop=(t == N - 1))
     mm.then_inc(S.ym, 1)
     ve.wait_ge(S.ym, 1)
     ve.tensor_copy(T.ysb[:, :], T.yp[:, 0:QP]).then_inc(S.yc, 1)

@@ -1,46 +1,32 @@
 from concourse.bass import DstId, RemoteDMATransfer
-from concourse.mybir import AluOpType
+from concourse.mybir import AluOpType, AxisListType, ActivationFunctionType
 
 N, QP, KP = 6, 32, 128
-W = 2 * KP
-HN = N // 2
-HC = HN * QP
+MB = 8
+RANGE = [(0, 3), (0, 2), (2, 3)]
 
 SCRATCH = {
-    "kv": ("sbuf", [128, N * W], "bfloat16"),
-    "qs": ("sbuf", [128, QP], "bfloat16"),
-    "erow": ("sbuf", [128, QP * QP], "bfloat16"),
-    "zero": ("sbuf", [128, KP], "bfloat16"),
-    "nh": ("sbuf", [128, KP], "bfloat16"),
-    "eye3": ("sbuf", [128, HC], "bfloat16"),
-    "tr": ("sbuf", [128, 192], "float32"),
-    "mcol": ("sbuf", [128, 8], "bfloat16"),
-    "mrow": ("sbuf", [128, HC], "bfloat16"),
-    "pp": ("sbuf", [128, 2 * HC], "bfloat16"),
-    "ysb": ("sbuf", [128, QP], "bfloat16"),
-    "sp0": ("psum", [128, 512], "float32"),
-    "sp1": ("psum", [128, 512], "float32"),
-    "yp": ("psum", [128, 512], "float32"),
+    "qw": ("sbuf", [128, 3 * QP], "bfloat16"),
+    "kk": ("sbuf", [128, 4 * KP], "bfloat16"),
+    "vv": ("sbuf", [128, N * KP], "bfloat16"),
+    "ones": ("sbuf", [128, 128], "bfloat16"),
+    "zero": ("sbuf", [128, 128], "bfloat16"),
+    "eye": ("sbuf", [128, 128], "bfloat16"),
+    "eyer": ("sbuf", [128, 128], "bfloat16"),
+    "sg": ("sbuf", [128, 4 * QP + MB], "bfloat16"),
+    "sr": ("sbuf", [128, 4 * QP + MB], "bfloat16"),
+    "mo": ("sbuf", [128, 8], "bfloat16"),
+    "sc": ("sbuf", [128, 8], "bfloat16"),
+    "dg": ("sbuf", [128, 128], "bfloat16"),
+    "pp": ("sbuf", [128, N * QP], "bfloat16"),
+    "yo": ("sbuf", [128, QP], "bfloat16"),
 }
-for _j in range(1, N):
-    SCRATCH["st%d" % _j] = ("psum", [128, 512], "float32")
+for _b in range(8):
+    SCRATCH["b%d" % _b] = ("psum", [128, 512], "float32")
 
-SEMAPHORES = ["ldk", "ldv", "ldq", "sent", "c0", "cs", "zi", "im", "ic", "sa", "vx", "mx", "rw", "rc", "b0", "b1", "r0",
-              "r1", "ym", "yc", "out"] + [p + str(j) for p in ("arr", "ka", "va", "st") for j in range(N)]
-
-
-def _kc(j):
-    b = (j // 2) * 2 * W
-    return (b, b + KP) if j % 2 == 0 else (b + 3 * KP, b + 4 * KP)
-
-
-def _vc(j):
-    b = (j // 2) * 2 * W
-    return (b + KP, b + 2 * KP) if j % 2 == 0 else (b + 2 * KP, b + 3 * KP)
-
-
-def _sc(j):
-    return (min(_kc(j)[0], _vc(j)[0]), max(_kc(j)[1], _vc(j)[1]))
+SEMAPHORES = (["ldq", "ldk", "ldv", "sent", "cs", "ey", "zi", "sa", "gs", "cg", "mo", "rm", "dd", "sb0", "sb1", "pr0", "pr1", "ym",
+               "yc", "out", "sx", "vp"] + [p + str(t) for p in ("ts", "rl", "ka", "va") for t in range(4)]
+              + [p + str(i) for p in ("qa", "vf") for i in range(3)])
 
 
 def _place(topo, c):
@@ -60,48 +46,22 @@ def _plan(topo, cores):
     groups = {}
     for c in cores:
         groups.setdefault(_place(topo, c), []).append(c)
-    rk = {c: i for i, c in enumerate(cores)}
-    sends, kr, vr, far, fwd, nearr, restm = {}, {}, {}, {}, {}, {}, {}
-    for c in cores:
-        kr[c], vr[c], far[c], fwd[c], nearr[c] = {rk[c]: ("ldk", 16)}, {rk[c]: ("ldv", 16)}, [], [], []
-    for c in cores:
-        L = groups[_place(topo, c)]
-        G = [x for x in cores if x not in L]
-        i, a, b, r = L.index(c), len(L), len(G), rk[c]
-        near = L[i + 1:] + L[:i]
-        full = topo.mask(c, near[0])
-        off = full & topo.mask(c, G[0])
-        rest = full & ~off
-        restm[c] = rest
-        tg = [G[x] for x in range(b) if x % a == i] if a <= b else [G[i // (a // b)]]
-        sends[c] = [([("ldk", 16), ("ldv", 16)], [(rest, near, _sc(r), "arr%d" % r)]),
-                    ([], [(off, tg, _kc(r), "ka%d" % r)]),
-                    ([], [(off, tg, _vc(r), "va%d" % r)])]
-        for d in tg:
-            kr[d][r], vr[d][r] = ("ka%d" % r, _bits(off)), ("va%d" % r, _bits(off))
-            far[d].append(r)
-        for d in near:
-            kr[d][r] = vr[d][r] = ("arr%d" % r, _bits(rest))
-            nearr[d].append(r)
-    for c in cores:
-        L = groups[_place(topo, c)]
-        held = sorted(far[c])
-        who = {}
-        for r in held:
-            holders = [x for x in L if r in far[x]]
-            lacking = [x for x in L if r not in far[x]]
-            who[r] = lacking[holders.index(c)::len(holders)]
-        rest = restm[c]
-        masks = [rest] if len(held) == 1 else list(_halves(rest))
-        sends[c].append(([kr[c][r] for r in held], [(masks[t], who[r], _kc(r), "ka%d" % r) for t, r in enumerate(held)]))
-        cols = (min(_vc(r)[0] for r in held), max(_vc(r)[1] for r in held))
-        sends[c].append(([vr[c][r] for r in held], [(rest, who[held[0]], cols, "va%d" % held[0])]))
-        for t, r in enumerate(held):
-            for d in who[r]:
-                kr[d][r], vr[d][r] = ("ka%d" % r, _bits(masks[t])), ("va%d" % held[0], _bits(rest))
-                fwd[d].append(r)
-    order = {c: [rk[c]] + nearr[c] + far[c] + fwd[c] for c in cores}
-    return sends, kr, vr, order
+    small, big = sorted(groups.values(), key=len)
+    per = len(big) // len(small)
+    info = {}
+    for j, s in enumerate(small):
+        members = [s] + big[per * j:per * (j + 1)]
+        for i, c in enumerate(members):
+            L = small if i == 0 else big
+            x = L.index(c)
+            near = L[x + 1:] + L[:x]
+            full = topo.mask(c, near[0])
+            off = full & topo.mask(c, members[1 if i == 0 else 0])
+            n_off = len(near) // 3
+            info[c] = {"members": members, "mi": i, "L": L, "li": x, "off": off, "rest": full & ~off, "near": near,
+                       "on_rest": near[:len(near) - n_off], "on_off": near[len(near) - n_off:],
+                       "order": [x] + [z for z in range(len(L)) if z != x]}
+    return info
 
 
 def rank_program(g, core, T, topo):
@@ -109,107 +69,150 @@ def rank_program(g, core, T, topo):
     if rank is None:
         return
     cores = list(T.cores)
+    rk = {c: i for i, c in enumerate(cores)}
     S = T.sem
-    te, ve = g.tensor, g.vector
-    mx_op = AluOpType.max
-    sends, kr, vr, order = _plan(topo, cores)
-    sends, kr, vr, order = sends[core], kr[core], vr[core], order[core]
-    sp = [T.sp0, T.sp1]
+    te, ve, ac = g.tensor, g.vector, g.scalar
+    mx = AluOpType.max
+    info = _plan(topo, cores)
+    me = info[core]
+    members, mi, L, li, off, rest, order = (me["members"], me["mi"], me["L"], me["li"], me["off"], me["rest"], me["order"])
+    nk = len(L)
+    b0, b1 = RANGE[mi]
+    p0, p1 = QP * b0, QP * b1
+    o0, o1 = QP * mi, QP * (mi + 1)
+    guests = [i for i in range(b0, b1) if i != mi]
+    partner = members[1 if mi == 0 else 0]
+    pa = info[partner]
+    nkp = len(pa["L"])
+    twin = [c for c in cores if info[c]["mi"] == mi and c != core][0]
+    gw, wS = nk * QP, nkp * QP
+    second = (mi == 2)
+    st, gp, sp0, sp1, yp = [T.b0, T.b1, T.b2, T.b3], [T.b4, T.b3], T.b5, T.b6, T.b7
+    qmine, qall = T.qw[:, o0:o1], T.qw[:, p0:p1]
 
-    def cols(cc):
-        return T.kv[:, cc[0]:cc[1]]
+    def sl(buf, s):
+        return buf[:, KP * s:KP * (s + 1)]
 
-    g.sync.dma_start(cols(_kc(rank)), T.k[:, :]).then_inc(S.ldk, 16)
-    g.scalar.dma_start(cols(_vc(rank)), T.v[:, :]).then_inc(S.ldv, 16)
-    g.sync.dma_start(T.qs[:, :], T.q[:, :]).then_inc(S.ldq, 16)
+    sent = [0]
 
-    sent = 0
-    for waits, transfers in sends:
-        for s, n in waits:
-            g.wait_ge(S[s], n)
-        trs = []
-        for m, dsts, cc, s in transfers:
-            ids = []
-            for d in dsts:
-                rid, pid = topo.addr(d, core)
-                ids.append(DstId(rid=rid, pnc=pid))
-            trs.append(RemoteDMATransfer(dst_ids=ids, dma_engine_mask=m, remote_sem=S[s], srcs=[cols(cc)],
-                                         dsts=[cols(cc) for _ in dsts], alu_op=0))
-            sent += _bits(m)
-        g.remote_dma_fused(trs, local_sem=S.sent)
+    def tr(mask, dsts, src, dst, sem):
+        ids = []
+        for d in dsts:
+            rid, pid = topo.addr(d, core)
+            ids.append(DstId(rid=rid, pnc=pid))
+        sent[0] += _bits(mask)
+        return RemoteDMATransfer(dst_ids=ids, dma_engine_mask=mask, remote_sem=sem, srcs=[src],
+                                 dsts=[dst for _ in dsts], alu_op=0)
 
-    ve.memset(T.erow[0:1, :], 0.0).then_inc(S.c0, 1)
-    ve.memset(T.zero[:, :], 0.0).then_inc(S.cs, 1)
-    ve.memset(T.nh[0:1, :], -0.5).then_inc(S.cs, 1)
-    ve.wait_ge(S.c0, 1)
-    ve.memset(T.erow[0:1, 0:QP * QP:QP + 1], 1.0).then_inc(S.cs, 1)
+    g.sync.dma_start(qmine, T.q[:, :]).then_inc(S.ldq, 16)
+    ac.dma_start(sl(T.kk, li), T.k[:, :]).then_inc(S.ldk, 16)
+    g.sync.dma_start(sl(T.vv, rank), T.v[:, :]).then_inc(S.ldv, 16)
+
+    ve.memset(T.zero[0:1, :], 0.0).then_inc(S.cs, 1)
+    ve.memset(T.ones[:, :], 1.0).then_inc(S.cs, 1)
+    ve.memset(T.sg[:, gw:gw + MB], 0.0).then_inc(S.cs, 1)
     ve.wait_ge(S.cs, 3)
 
+    g.wait_ge(S.ldq, 16)
+    g.remote_dma_fused([tr(off, [partner], qmine, qmine, S["qa%d" % mi])], local_sem=S.sent)
+    g.wait_ge(S.ldk, 16)
+    trs = [tr(rest, me["on_rest"], sl(T.kk, li), sl(T.kk, li), S["ka%d" % li])]
+    if me["on_off"]:
+        trs.append(tr(off, me["on_off"], sl(T.kk, li), sl(T.kk, li), S["ka%d" % li]))
+    g.remote_dma_fused(trs, local_sem=S.sent)
+    g.wait_ge(S.ldv, 16)
+    g.remote_dma_fused([tr(off, members[1:] if mi == 0 else [members[0]], sl(T.vv, rank), sl(T.vv, rank), S["vf%d" % mi]),
+                        tr(rest, me["near"], sl(T.vv, rank), sl(T.vv, rank), S["va%d" % li])], local_sem=S.sent)
+    g.wait_ge(S.cs, 3)
+    g.affine_select(T.eyer[:, :], T.ones[:, :], [[0, 4], [-1, QP]], AluOpType.is_equal, 0.0, -o0, 1).then_inc(S.ey, 1)
+    g.affine_select(T.eye[:, :], T.ones[:, :], [[-1, 128]], AluOpType.is_equal, 0.0, 0, 1).then_inc(S.ey, 1)
+
     te.wait_ge(S.cs, 3)
-    for h in range(2):
-        te.matmul(sp[h][:, 0:HC], T.zero[0:1, 0:KP], T.zero[0:1, 0:HC], start=True, stop=False).then_inc(S.zi, 1)
-    for i in range(QP):
-        e = T.erow[0:1, QP * i:QP * (i + 1)]
-        mm = te.matmul(T.yp[0:QP, 0:QP], e, e, start=(i == 0), stop=(i == QP - 1))
-    mm.then_inc(S.im, 1)
-    ve.wait_ge(S.im, 1)
-    for j in range(HN):
-        ve.tensor_copy(T.eye3[0:QP, QP * j:QP * (j + 1)], T.yp[0:QP, 0:QP]).then_inc(S.ic, 1)
-
-    te.wait_ge(S.zi, 2)
-    te.wait_ge(S.ic, HN)
+    te.matmul(sp0[:, 0:gw], T.zero[0:1, 0:KP], T.zero[0:1, 0:gw], start=True, stop=False).then_inc(S.zi, 1)
+    te.wait_ge(S.zi, 1)
     te.wait_ge(S.ldq, 16)
-    H = KP // 2
-    halves = [T.tr[0:QP, 0:H], T.tr[0:QP, H:2 * H]]
-    nv = 0
-    for t, j in enumerate(order):
-        te.wait_ge(S[kr[j][0]], kr[j][1])
-        st = T.yp if t == 0 else T["st%d" % t]
-        c0 = QP * (t % HN)
-        te.matmul(st[0:QP, 0:KP], T.qs[:, :], cols(_kc(j)), start=True, stop=True).then_inc(S["st%d" % t], 1)
-        te.matmul(sp[t // HN][:, c0:c0 + QP], cols(_kc(j)), T.qs[:, :], start=False, stop=False).then_inc(S.sa, 1)
-        ve.wait_ge(S["st%d" % t], 1)
-        for h in range(2):
-            part = st[0:QP, H * h:H * (h + 1)]
-            if nv == 0:
-                ve.tensor_copy(halves[0], part).then_inc(S.vx, 1)
-            else:
-                ve.wait_ge(S.vx, nv)
-                ve.tensor_tensor(halves[nv % 2], part, halves[(nv - 1) % 2], mx_op).then_inc(S.vx, 1)
-            nv += 1
-    width, base = H, 2 * H
-    cur_lo = ((nv - 1) % 2) * H
-    while width > 1:
-        width //= 2
-        ve.wait_ge(S.vx, nv)
-        a = T.tr[0:QP, cur_lo:cur_lo + width]
-        b = T.tr[0:QP, cur_lo + width:cur_lo + 2 * width]
-        if width > 1:
-            ve.tensor_tensor(T.tr[0:QP, base:base + width], a, b, mx_op).then_inc(S.vx, 1)
-            nv += 1
-            cur_lo, base = base, base + width
+    for i in guests:
+        te.wait_ge(S["qa%d" % i], _bits(info[members[i]]["off"]))
+    for t, s in enumerate(order):
+        if s == li:
+            te.wait_ge(S.ldk, 16)
         else:
-            ve.tensor_tensor(T.mcol[0:QP, 0:1], a, b, mx_op).then_inc(S.mx, 1)
+            o = info[L[s]]
+            te.wait_ge(S["ka%d" % s], _bits(o["rest"] if core in o["on_rest"] else o["off"]))
+        te.matmul(st[t][p0:p1, 0:KP], qall, sl(T.kk, s), start=True, stop=True).then_inc(S["ts%d" % t], 1)
+        for x, i in enumerate(guests):
+            te.matmul(gp[x][:, QP * t:QP * (t + 1)], sl(T.kk, s), T.qw[:, QP * i:QP * (i + 1)], start=True,
+                      stop=True).then_inc(S.gs, 1)
+        te.matmul(sp0[:, QP * t:QP * (t + 1)], sl(T.kk, s), qmine, start=False, stop=False).then_inc(S.sa, 1)
+        ve.wait_ge(S["ts%d" % t], 1)
+        ve.tensor_reduce(T.sg[p0:p1, gw + t:gw + t + 1], st[t][p0:p1, 0:KP], AxisListType.X, mx).then_inc(S["rl%d" % t], 1)
 
-    te.wait_ge(S.mx, 1)
-    te.matmul(T.st1[0:1, 0:HC], T.mcol[0:QP, 0:1], T.eye3[0:QP, 0:HC], start=True, stop=True).then_inc(S.rw, 1)
-    ve.wait_ge(S.rw, 1)
-    ve.tensor_copy(T.mrow[0:1, 0:HC], T.st1[0:1, 0:HC]).then_inc(S.rc, 1)
-    te.wait_ge(S.rc, 1)
-    te.wait_ge(S.sa, N)
-    for h in range(2):
-        te.matmul(sp[h][:, 0:HC], T.nh[0:1, 0:KP], T.mrow[0:1, 0:HC], start=False, stop=True).then_inc(S["b%d" % h], 1)
-        ve.wait_ge(S["b%d" % h], 1)
-        ve.tensor_tensor(T.pp[:, HC * h:HC * (h + 1)], sp[h][:, 0:HC], T.zero[:, 0:HC], mx_op).then_inc(S["r%d" % h], 1)
-    for t, j in enumerate(order):
-        if t % HN == 0:
-            te.wait_ge(S["r%d" % (t // HN)], 1)
-        te.wait_ge(S[vr[j][0]], vr[j][1])
-        mm = te.matmul(T.yp[:, 0:QP], cols(_vc(j)), T.pp[:, QP * t:QP * (t + 1)], start=(t == 0), stop=(t == N - 1))
+    if guests:
+        ac.wait_ge(S.gs, nk * len(guests))
+        for x in range(len(guests)):
+            c = x * (gw + MB)
+            ac.activation(T.sg[:, c:c + gw], gp[x][:, 0:gw], ActivationFunctionType.Copy).then_inc(S.cg, 1)
+        for t in range(nk):
+            g.wait_ge(S["rl%d" % t], 1)
+        g.wait_ge(S.cg, len(guests))
+        masks = [off] if len(guests) == 1 else list(_halves(off))
+        g.remote_dma_fused([tr(masks[x], [members[i]], T.sg[:, x * gw:x * gw + gw + MB], T.sr[:, 0:gw + MB], S.sx)
+                            for x, i in enumerate(guests)], local_sem=S.sent)
+
+    got = members[1:] if mi == 0 else [members[0]]
+    for c in got:
+        g.wait_ge(S["vf%d" % info[c]["mi"]], _bits(info[c]["off"]))
+    vcols = T.vv[:, KP * min(rk[c] for c in got):KP * (max(rk[c] for c in got) + 1)]
+    g.remote_dma_fused([tr(rest, [twin], vcols, vcols, S.vp)], local_sem=S.sent)
+
+    for t in range(nk):
+        ve.wait_ge(S["rl%d" % t], 1)
+    ve.tensor_reduce(T.mo[o0:o1, 0:1], T.sg[o0:o1, gw:gw + nk], AxisListType.X, mx).then_inc(S.mo, 1)
+    ve.wait_ge(S.mo, 1)
+    ve.wait_ge(S.ey, 2)
+    nsx = _bits(pa["off"]) if mi == 0 else _bits(_halves(pa["off"])[0])
+    m0, s0 = (0, MB) if second else (wS, 0)
+    ve.wait_ge(S.sx, nsx)
+    rec = T.sr[o0:o1, m0:m0 + nkp]
+    ve.tensor_tensor_scan(T.sc[o0:o1, 0:nkp], rec, rec, T.mo[o0:o1, 0:1], mx, mx).then_inc(S.rm, 1)
+    ve.wait_ge(S.rm, 1)
+    ve.tensor_scalar(T.dg[o0:o1, :], T.eyer[o0:o1, :], T.sc[o0:o1, nkp - 1:nkp], -0.5, AluOpType.mult,
+                     AluOpType.mult).then_inc(S.dd, 1)
+    te.wait_ge(S.ey, 2)
+    te.wait_ge(S.sx, nsx)
+    te.matmul(sp1[:, 0:wS], T.eye[:, :], T.sr[:, s0:s0 + wS], start=True, stop=False)
+    te.wait_ge(S.sa, nk)
+    te.wait_ge(S.dd, 1)
+    te.matmul(sp0[:, 0:gw], T.ones[o0:o1, 0:KP], T.dg[o0:o1, 0:gw], start=False, stop=True).then_inc(S.sb0, 1)
+    te.matmul(sp1[:, 0:wS], T.ones[o0:o1, 0:KP], T.dg[o0:o1, 0:wS], start=False, stop=True).then_inc(S.sb1, 1)
+    ac.wait_ge(S.sb0, 1)
+    ac.activation(T.pp[:, 0:gw], sp0[:, 0:gw], ActivationFunctionType.Relu).then_inc(S.pr0, 1)
+    ve.wait_ge(S.sb1, 1)
+    ve.tensor_scalar(T.pp[:, gw:gw + wS], sp1[:, 0:wS], 0.0, None, mx).then_inc(S.pr1, 1)
+
+    items = []
+    for t, s in enumerate(order):
+        c = L[s]
+        items.append((0 if c == core else 1, t, rk[c], "ldv" if c == core else "va%d" % s, 16 if c == core else _bits(info[c]["rest"])))
+    for u, s in enumerate(pa["order"]):
+        c = pa["L"][s]
+        if c in members:
+            items.append((2, nk + u, rk[c], "vf%d" % info[c]["mi"], _bits(info[c]["off"])))
+        else:
+            items.append((3, nk + u, rk[c], "vp", _bits(info[twin]["rest"])))
+    items.sort()
+    te.wait_ge(S.pr0, 1)
+    far_seen = False
+    for n, (cl, pos, r, sem, cnt) in enumerate(items):
+        if cl >= 2 and not far_seen:
+            te.wait_ge(S.pr1, 1)
+            far_seen = True
+        te.wait_ge(S[sem], cnt)
+        mm = te.matmul(yp[:, 0:QP], sl(T.vv, r), T.pp[:, QP * pos:QP * (pos + 1)], start=(n == 0), stop=(n == N - 1))
     mm.then_inc(S.ym, 1)
     ve.wait_ge(S.ym, 1)
-    ve.tensor_copy(T.ysb[:, :], T.yp[:, 0:QP]).then_inc(S.yc, 1)
+    ve.tensor_copy(T.yo[:, :], yp[:, 0:QP]).then_inc(S.yc, 1)
     g.sync.wait_ge(S.yc, 1)
-    g.sync.dma_start(T.y[:, :], T.ysb[:, :]).then_inc(S.out, 16)
+    g.sync.dma_start(T.y[:, :], T.yo[:, :]).then_inc(S.out, 16)
     g.sync.wait_ge(S.out, 16)
-    g.wait_ge(S.sent, sent)
+    g.wait_ge(S.sent, sent[0])

from concourse.bass import DstId, RemoteDMATransfer
from concourse.mybir import AluOpType, AxisListType, ActivationFunctionType

N, QP, KP = 6, 32, 128
MB = 8
RANGE = [(0, 3), (0, 2), (2, 3)]

SCRATCH = {
    "qw": ("sbuf", [128, 3 * QP], "bfloat16"),
    "kk": ("sbuf", [128, 4 * KP], "bfloat16"),
    "vv": ("sbuf", [128, N * KP], "bfloat16"),
    "ones": ("sbuf", [128, 128], "bfloat16"),
    "zero": ("sbuf", [128, 128], "bfloat16"),
    "eye": ("sbuf", [128, 128], "bfloat16"),
    "eyer": ("sbuf", [128, 128], "bfloat16"),
    "sg": ("sbuf", [128, 4 * QP + MB], "bfloat16"),
    "sr": ("sbuf", [128, 4 * QP + MB], "bfloat16"),
    "mo": ("sbuf", [128, 8], "bfloat16"),
    "sc": ("sbuf", [128, 8], "bfloat16"),
    "dg": ("sbuf", [128, 128], "bfloat16"),
    "pp": ("sbuf", [128, N * QP], "bfloat16"),
    "yo": ("sbuf", [128, QP], "bfloat16"),
}
for _b in range(8):
    SCRATCH["b%d" % _b] = ("psum", [128, 512], "float32")

SEMAPHORES = (["ldq", "ldk", "ldv", "sent", "cs", "ey", "zi", "sa", "gs", "cg", "mo", "rm", "dd", "sb0", "sb1", "pr0", "pr1", "ym",
               "yc", "out", "sx", "vp"] + [p + str(t) for p in ("ts", "rl", "ka", "va") for t in range(4)]
              + [p + str(i) for p in ("qa", "vf") for i in range(3)])


def _place(topo, c):
    return (topo.host(c), topo.chip(c))


def _bits(m):
    return bin(m).count("1")


def _halves(m):
    e = [1 << x for x in range(m.bit_length()) if (m >> x) & 1]
    return sum(e[:len(e) // 2]), sum(e[len(e) // 2:])


def _plan(topo, cores):
    groups = {}
    for c in cores:
        groups.setdefault(_place(topo, c), []).append(c)
    small, big = sorted(groups.values(), key=len)
    per = len(big) // len(small)
    info = {}
    for j, s in enumerate(small):
        members = [s] + big[per * j:per * (j + 1)]
        for i, c in enumerate(members):
            L = small if i == 0 else big
            x = L.index(c)
            near = L[x + 1:] + L[:x]
            full = topo.mask(c, near[0])
            off = full & topo.mask(c, members[1 if i == 0 else 0])
            n_off = len(near) // 3
            info[c] = {"members": members, "mi": i, "L": L, "li": x, "off": off, "rest": full & ~off, "near": near,
                       "on_rest": near[:len(near) - n_off], "on_off": near[len(near) - n_off:],
                       "order": [x] + [z for z in range(len(L)) if z != x]}
    return info


def rank_program(g, core, T, topo):
    rank = T.rank_of(core)
    if rank is None:
        return
    cores = list(T.cores)
    rk = {c: i for i, c in enumerate(cores)}
    S = T.sem
    te, ve, ac = g.tensor, g.vector, g.scalar
    mx = AluOpType.max
    info = _plan(topo, cores)
    me = info[core]
    members, mi, L, li, off, rest, order = (me["members"], me["mi"], me["L"], me["li"], me["off"], me["rest"], me["order"])
    nk = len(L)
    b0, b1 = RANGE[mi]
    p0, p1 = QP * b0, QP * b1
    o0, o1 = QP * mi, QP * (mi + 1)
    guests = [i for i in range(b0, b1) if i != mi]
    partner = members[1 if mi == 0 else 0]
    pa = info[partner]
    nkp = len(pa["L"])
    twin = [c for c in cores if info[c]["mi"] == mi and c != core][0]
    gw, wS = nk * QP, nkp * QP
    second = (mi == 2)
    st, gp, sp0, sp1, yp = [T.b0, T.b1, T.b2, T.b3], [T.b4, T.b3], T.b5, T.b6, T.b7
    qmine, qall = T.qw[:, o0:o1], T.qw[:, p0:p1]

    def sl(buf, s):
        return buf[:, KP * s:KP * (s + 1)]

    sent = [0]

    def tr(mask, dsts, src, dst, sem):
        ids = []
        for d in dsts:
            rid, pid = topo.addr(d, core)
            ids.append(DstId(rid=rid, pnc=pid))
        sent[0] += _bits(mask)
        return RemoteDMATransfer(dst_ids=ids, dma_engine_mask=mask, remote_sem=sem, srcs=[src],
                                 dsts=[dst for _ in dsts], alu_op=0)

    g.sync.dma_start(qmine, T.q[:, :]).then_inc(S.ldq, 16)
    ac.dma_start(sl(T.kk, li), T.k[:, :]).then_inc(S.ldk, 16)
    g.sync.dma_start(sl(T.vv, rank), T.v[:, :]).then_inc(S.ldv, 16)

    ve.memset(T.zero[0:1, :], 0.0).then_inc(S.cs, 1)
    ve.memset(T.ones[:, :], 1.0).then_inc(S.cs, 1)
    ve.memset(T.sg[:, gw:gw + MB], 0.0).then_inc(S.cs, 1)
    ve.wait_ge(S.cs, 3)

    g.wait_ge(S.ldq, 16)
    g.remote_dma_fused([tr(off, [partner], qmine, qmine, S["qa%d" % mi])], local_sem=S.sent)
    g.wait_ge(S.ldk, 16)
    trs = [tr(rest, me["on_rest"], sl(T.kk, li), sl(T.kk, li), S["ka%d" % li])]
    if me["on_off"]:
        trs.append(tr(off, me["on_off"], sl(T.kk, li), sl(T.kk, li), S["ka%d" % li]))
    g.remote_dma_fused(trs, local_sem=S.sent)
    g.wait_ge(S.ldv, 16)
    g.remote_dma_fused([tr(off, members[1:] if mi == 0 else [members[0]], sl(T.vv, rank), sl(T.vv, rank), S["vf%d" % mi]),
                        tr(rest, me["near"], sl(T.vv, rank), sl(T.vv, rank), S["va%d" % li])], local_sem=S.sent)
    g.wait_ge(S.cs, 3)
    g.affine_select(T.eyer[:, :], T.ones[:, :], [[0, 4], [-1, QP]], AluOpType.is_equal, 0.0, -o0, 1).then_inc(S.ey, 1)
    g.affine_select(T.eye[:, :], T.ones[:, :], [[-1, 128]], AluOpType.is_equal, 0.0, 0, 1).then_inc(S.ey, 1)

    te.wait_ge(S.cs, 3)
    te.matmul(sp0[:, 0:gw], T.zero[0:1, 0:KP], T.zero[0:1, 0:gw], start=True, stop=False).then_inc(S.zi, 1)
    te.wait_ge(S.zi, 1)
    te.wait_ge(S.ldq, 16)
    for i in guests:
        te.wait_ge(S["qa%d" % i], _bits(info[members[i]]["off"]))
    for t, s in enumerate(order):
        if s == li:
            te.wait_ge(S.ldk, 16)
        else:
            o = info[L[s]]
            te.wait_ge(S["ka%d" % s], _bits(o["rest"] if core in o["on_rest"] else o["off"]))
        te.matmul(st[t][p0:p1, 0:KP], qall, sl(T.kk, s), start=True, stop=True).then_inc(S["ts%d" % t], 1)
        for x, i in enumerate(guests):
            te.matmul(gp[x][:, QP * t:QP * (t + 1)], sl(T.kk, s), T.qw[:, QP * i:QP * (i + 1)], start=True,
                      stop=True).then_inc(S.gs, 1)
        te.matmul(sp0[:, QP * t:QP * (t + 1)], sl(T.kk, s), qmine, start=False, stop=False).then_inc(S.sa, 1)
        ve.wait_ge(S["ts%d" % t], 1)
        ve.tensor_reduce(T.sg[p0:p1, gw + t:gw + t + 1], st[t][p0:p1, 0:KP], AxisListType.X, mx).then_inc(S["rl%d" % t], 1)

    if guests:
        ac.wait_ge(S.gs, nk * len(guests))
        for x in range(len(guests)):
            c = x * (gw + MB)
            ac.activation(T.sg[:, c:c + gw], gp[x][:, 0:gw], ActivationFunctionType.Copy).then_inc(S.cg, 1)
        for t in range(nk):
            g.wait_ge(S["rl%d" % t], 1)
        g.wait_ge(S.cg, len(guests))
        masks = [off] if len(guests) == 1 else list(_halves(off))
        g.remote_dma_fused([tr(masks[x], [members[i]], T.sg[:, x * gw:x * gw + gw + MB], T.sr[:, 0:gw + MB], S.sx)
                            for x, i in enumerate(guests)], local_sem=S.sent)

    got = members[1:] if mi == 0 else [members[0]]
    for c in got:
        g.wait_ge(S["vf%d" % info[c]["mi"]], _bits(info[c]["off"]))
    vcols = T.vv[:, KP * min(rk[c] for c in got):KP * (max(rk[c] for c in got) + 1)]
    g.remote_dma_fused([tr(rest, [twin], vcols, vcols, S.vp)], local_sem=S.sent)

    for t in range(nk):
        ve.wait_ge(S["rl%d" % t], 1)
    ve.tensor_reduce(T.mo[o0:o1, 0:1], T.sg[o0:o1, gw:gw + nk], AxisListType.X, mx).then_inc(S.mo, 1)
    ve.wait_ge(S.mo, 1)
    ve.wait_ge(S.ey, 2)
    nsx = _bits(pa["off"]) if mi == 0 else _bits(_halves(pa["off"])[0])
    m0, s0 = (0, MB) if second else (wS, 0)
    ve.wait_ge(S.sx, nsx)
    rec = T.sr[o0:o1, m0:m0 + nkp]
    ve.tensor_tensor_scan(T.sc[o0:o1, 0:nkp], rec, rec, T.mo[o0:o1, 0:1], mx, mx).then_inc(S.rm, 1)
    ve.wait_ge(S.rm, 1)
    ve.tensor_scalar(T.dg[o0:o1, :], T.eyer[o0:o1, :], T.sc[o0:o1, nkp - 1:nkp], -0.5, AluOpType.mult,
                     AluOpType.mult).then_inc(S.dd, 1)
    te.wait_ge(S.ey, 2)
    te.wait_ge(S.sx, nsx)
    te.matmul(sp1[:, 0:wS], T.eye[:, :], T.sr[:, s0:s0 + wS], start=True, stop=False)
    te.wait_ge(S.sa, nk)
    te.wait_ge(S.dd, 1)
    te.matmul(sp0[:, 0:gw], T.ones[o0:o1, 0:KP], T.dg[o0:o1, 0:gw], start=False, stop=True).then_inc(S.sb0, 1)
    te.matmul(sp1[:, 0:wS], T.ones[o0:o1, 0:KP], T.dg[o0:o1, 0:wS], start=False, stop=True).then_inc(S.sb1, 1)
    ac.wait_ge(S.sb0, 1)
    ac.activation(T.pp[:, 0:gw], sp0[:, 0:gw], ActivationFunctionType.Relu).then_inc(S.pr0, 1)
    ve.wait_ge(S.sb1, 1)
    ve.tensor_scalar(T.pp[:, gw:gw + wS], sp1[:, 0:wS], 0.0, None, mx).then_inc(S.pr1, 1)

    items = []
    for t, s in enumerate(order):
        c = L[s]
        items.append((0 if c == core else 1, t, rk[c], "ldv" if c == core else "va%d" % s, 16 if c == core else _bits(info[c]["rest"])))
    for u, s in enumerate(pa["order"]):
        c = pa["L"][s]
        if c in members:
            items.append((2, nk + u, rk[c], "vf%d" % info[c]["mi"], _bits(info[c]["off"])))
        else:
            items.append((3, nk + u, rk[c], "vp", _bits(info[twin]["rest"])))
    items.sort()
    te.wait_ge(S.pr0, 1)
    far_seen = False
    for n, (cl, pos, r, sem, cnt) in enumerate(items):
        if cl >= 2 and not far_seen:
            te.wait_ge(S.pr1, 1)
            far_seen = True
        te.wait_ge(S[sem], cnt)
        mm = te.matmul(yp[:, 0:QP], sl(T.vv, r), T.pp[:, QP * pos:QP * (pos + 1)], start=(n == 0), stop=(n == N - 1))
    mm.then_inc(S.ym, 1)
    ve.wait_ge(S.ym, 1)
    ve.tensor_copy(T.yo[:, :], yp[:, 0:QP]).then_inc(S.yc, 1)
    g.sync.wait_ge(S.yc, 1)
    g.sync.dma_start(T.y[:, :], T.yo[:, :]).then_inc(S.out, 16)
    g.sync.wait_ge(S.out, 16)
    g.wait_ge(S.sent, sent[0])
